import numpy as np
import ml_dtypes


def mxq(x, axis, fmt="e4m3"):
    dtype, down = {"e4m3": (ml_dtypes.float8_e4m3fn, 7), "e5m2": (ml_dtypes.float8_e5m2, 14)}[fmt]
    v = np.moveaxis(np.asarray(x, np.float32).astype(ml_dtypes.bfloat16).astype(np.float64), axis, -1)
    blocks = v.reshape(v.shape[:-1] + (-1, 32))
    amax = np.abs(blocks).max(-1, keepdims=True)
    byte = np.maximum(np.where(amax > 0, np.frexp(amax)[1] - 1 + 127, 0) - down, 1)
    scale = np.exp2(byte - 127.0)
    codes = (blocks / scale).astype(np.float32).astype(dtype).astype(np.float64)
    return np.moveaxis((codes * scale).reshape(v.shape), -1, axis)


WIDE = False


def mx_kscale(k):
    if not WIDE:
        return np.ones(k)
    levels = np.array([10, -10, 5, -5, 0])
    if k % 512:
        return np.exp2(np.random.permutation(np.resize(levels, k // 32))).repeat(32)
    a = np.empty((k // 512, 16))
    for p in range(k // 512):
        a[p, :8] = np.random.permutation(np.resize(levels, 8))
        for g in range(8):
            far = levels[np.abs(levels - a[p, g]) >= 10]
            a[p, g + 8] = far[np.random.randint(len(far))]
    return np.exp2(a.ravel()).repeat(32)


def f64(x):
    return np.asarray(x).astype(np.float64)


def striped(idx):
    return np.tile(idx.reshape(-1, 16).T, (8, 1)).astype(np.uint16)


def unstriped(offs):
    return offs[:16].T.reshape(-1).astype(np.int64)


E2M1 = np.array([0.0, 0.5, 1.0, 1.5, 2.0, 3.0, 4.0, 6.0, -0.0, -0.5, -1.0, -1.5, -2.0, -3.0, -4.0, -6.0])


def pack_weight(w, fmt):
    k, n = w.shape
    w = f64(np.asarray(w, np.float32).astype(ml_dtypes.bfloat16)).reshape(k // 32, 32, n)
    amax = np.abs(w).max(1)
    if fmt == "e4m3":
        byte = np.frexp(amax)[1] - 1 + 127 - 7
    else:
        mant, ex = np.frexp(amax / 6.0)
        byte = np.where(mant > 0.5, ex, ex - 1) + 127
    byte = np.clip(np.where(amax > 0, byte, 1), 1, 254)
    scaled = (w * np.exp2(127.0 - byte)[:, None, :]).reshape(k, n).astype(np.float32)
    by_word = np.ascontiguousarray(scaled.reshape(k // 512, 128, 4, n).transpose(0, 1, 3, 2))
    if fmt == "e4m3":
        words = by_word.astype(ml_dtypes.float8_e4m3fn).view(np.uint8)
    else:
        c = by_word.astype(ml_dtypes.float4_e2m1fn).view(np.uint8) & 0xF
        words = (c[..., 0::2] | (c[..., 1::2] << 4)).reshape(k // 512, 128, 2 * n)
    return np.ascontiguousarray(words), np.ascontiguousarray(byte.astype(np.uint8).reshape(k // 512, 16, n))


def unpack_weight(words, scales, fmt):
    g, _, n = scales.shape
    words = np.ascontiguousarray(words).reshape(g, 128, n, -1)
    if fmt == "e4m3":
        vals = words.view(ml_dtypes.float8_e4m3fn).astype(np.float64)
    else:
        nib = np.empty((g, 128, n, 4), np.uint8)
        nib[..., 0::2] = words & 0xF
        nib[..., 1::2] = words >> 4
        vals = E2M1[nib]
    vals = vals * np.repeat(np.exp2(scales.astype(np.float64) - 127.0), 8, axis=1)[..., None]
    return vals.transpose(0, 1, 3, 2).reshape(g * 512, n)


def gelu(v):
    return 0.5 * v * (1.0 + np.tanh(np.sqrt(2.0 / np.pi) * (v + 0.044715 * v**3)))


K, T, S, H, T2, N, P = 1024, 2048, 1024, 1024, 2048, 512, 128

def setup_inputs():
    n = np.random.standard_normal
    s, u = mx_kscale(K)[:, None], mx_kscale(H)[:, None]
    tab_words, tab_scales = pack_weight(n((K, T)) * s, "e4m3")
    w4_words, w4_scales = pack_weight(n((K, H)) / np.sqrt(K) / s * u.T, "e2m1")
    return {
        "tab_words": tab_words, "tab_scales": tab_scales,
        "offs": striped(np.random.permutation(T)[:S]),
        "w4_words": w4_words, "w4_scales": w4_scales,
        "wgs": np.exp(0.3 * n((P, S))).astype(np.float32),
        "offs2": striped(np.random.permutation(T2)[:S]),
        "old": (n((H, T2)) * u).astype(np.float32),
        "dec": (n((H, N)) / np.sqrt(H) / u).astype(np.float32),
        "bd": (0.5 * n(N)).astype(np.float32),
    }

def reference(tab_words, tab_scales, offs, w4_words, w4_scales, wgs, offs2, old, dec, bd):
    v = unpack_weight(tab_words, tab_scales, "e4m3")[:, unstriped(offs)]
    w4 = unpack_weight(w4_words, w4_scales, "e2m1")
    h = w4.T @ v
    page = np.zeros((H, T2))
    page[:, unstriped(offs2)] = np.tile(f64(wgs), (H // P, 1)) * h
    z = mxq(f64(old) - page, 0, "e4m3")
    wd = mxq(f64(dec), 0, "e4m3")
    return (wd.T @ z) + f64(bd)[:, None]

@@ -1,0 +1,273 @@
+from contextlib import ExitStack
+
+import concourse.mybir as mybir
+from concourse.masks import make_identity
+
+K, T, S, H, T2, N = 1024, 2048, 1024, 1024, 2048, 512
+FLOPS = 2 * K * H * S + 2 * H * N * T2
+
+F32 = mybir.dt.float32
+BF16 = mybir.dt.bfloat16
+I32 = mybir.dt.int32
+U32 = mybir.dt.uint32
+U16 = mybir.dt.uint16
+U8 = mybir.dt.uint8
+FP8X4 = mybir.dt.float8_e4m3fn_x4
+FP4X4 = mybir.dt.float4_e2m1fn_x4
+MULT = mybir.AluOpType.mult
+ADD = mybir.AluOpType.add
+IDENT = mybir.ActivationFunctionType.Identity
+
+P = 128
+BANK = 512
+PASSES = 2
+SLICES = H // P
+CHUNKS = T2 // BANK
+NT = N // P
+
+
+def tile_list_sparse_optimiser_step_kernel(
+    tc, tab_words, tab_scales, offs, w4_words, w4_scales, wgs, offs2, old, dec, bd, out
+):
+    nc = tc.nc
+    with ExitStack() as ctx:
+        keep = ctx.enter_context(tc.tile_pool(name="keep", bufs=1))
+        rows = ctx.enter_context(tc.tile_pool(name="rows", bufs=3))
+        weave = ctx.enter_context(tc.tile_pool(name="weave", bufs=4))
+        psum = ctx.enter_context(tc.psum_pool(name="psum", bufs=1))
+
+        def kept(name, shape, dtype):
+            return keep.tile(shape, dtype, name=name, align_bytes=64)
+
+        banks = [psum.tile([P, BANK], F32, name=f"bank{b}") for b in range(8)]
+
+        pick = keep.tile([P, S // 16], U16, name="pick")
+        place = keep.tile([P, S // 16], U16, name="place")
+        tscale = keep.tile([P, T], U8, name="tscale", tag="early", align_bytes=64)
+        wscale = kept("wscale", [P, PASSES, H], U8)
+        vscale = [kept(f"vscale{a}", [P, S], U8) for a in range(PASSES)]
+        twords = [
+            rows.tile([P, T], U32, name="twords0", tag="rows", align_bytes=64),
+            keep.tile([P, T], U32, name="twords1", tag="late", align_bytes=64),
+        ]
+        picked = rows.tile([P, S], U8, name="picked", tag="rows", align_bytes=64)
+        wwords = rows.tile([P, PASSES, 2 * H], U8, name="wwords", tag="rows", align_bytes=64)
+        pages = [kept("page0", [P, T2], F32)]
+        ident = kept("ident", [P, P], F32)
+        bias = kept("bias", [P, NT], F32)
+        warm = kept("warm", [P, 16], F32)
+
+        nc.gpsimd.memset(warm[:], 0.0)
+        nc.scalar.activation(warm[:, 8:9], warm[:, 0:1], IDENT, scale=-1.0)
+        for q in range(4):
+            nc.vector.memset(tscale[32 * q : 32 * q + 24, :].bitcast(I32), 0)
+        nc.gpsimd.memset(wscale[:].rearrange("p a c -> p (a c)").bitcast(I32), 0)
+        for a in range(PASSES):
+            nc.gpsimd.memset(vscale[a][96:128, :].bitcast(I32), 0)
+        nc.vector.memset(pages[0][:], 0.0)
+        make_identity(nc, ident[:])
+
+        nc.sync.dma_start(pick[:], offs)
+        for q in range(4):
+            nc.sync.dma_start(
+                tscale[32 * q + 24 : 32 * q + 32, :].bitcast(I32), tab_scales[:, 4 * q : 4 * q + 4, :].bitcast(I32)
+            )
+        nc.sync.dma_start(twords[0][:].bitcast(I32), tab_words[0].rearrange("p t i -> p (t i)").bitcast(I32))
+        nc.sync.dma_start(place[:], offs2)
+        nc.sync.dma_start(twords[1][:].bitcast(I32), tab_words[1].rearrange("p t i -> p (t i)").bitcast(I32))
+        nc.sync.dma_start(wwords[:].bitcast(I32), w4_words.rearrange("a p c -> p a c").bitcast(I32))
+        steps = kept("steps", [P, S], F32)
+        nc.sync.dma_start(steps[:], wgs)
+        for q in range(4):
+            nc.scalar.dma_start(
+                wscale[32 * q : 32 * q + 4, :, :].bitcast(I32),
+                w4_scales[:, 4 * q : 4 * q + 4, :].rearrange("a r c -> r a c").bitcast(I32),
+            )
+
+        nc.vector.tensor_copy(picked[:], tscale[:].indirect(pick[:]))
+        vall = keep.tile([P, PASSES * S], U32, name="vwords", tag="early", align_bytes=64)
+        vwords = [[vall[:, S * a + BANK * i : S * a + BANK * (i + 1)] for i in range(2)] for a in range(PASSES)]
+        for a in range(PASSES):
+            first = 24 + 4 * a
+            nc.scalar.dma_start(vscale[a][0:100, :].bitcast(I32), picked[first : first + 100, :].bitcast(I32))
+        for i in range(2):
+            for a in range(PASSES):
+                nc.vector.tensor_copy(vwords[a][i], twords[a][:].indirect(pick[:, 32 * i : 32 * i + 32]))
+
+        pages.append(keep.tile([P, T2], F32, name="page1", tag="late", align_bytes=64))
+        nc.gpsimd.memset(pages[1][:], 0.0)
+        grads = [kept(f"grad{s}", [P, S], F32) for s in range(SLICES)]
+        for s in range(SLICES):
+            for i in range(2):
+                bank = banks[(2 * s + i) % 8]
+                cols = slice(BANK * i, BANK * (i + 1))
+                for a in range(PASSES):
+                    nc.tensor.matmul_mx(
+                        out=bank[:],
+                        lhsT=wwords[:, a, 2 * P * s : 2 * P * (s + 1)].bitcast(FP4X4),
+                        lhsT_scale=wscale[:, a, P * s : P * (s + 1)],
+                        rhs=vwords[a][i].bitcast(FP8X4),
+                        rhs_scale=vscale[a][:, cols],
+                        start=(a == 0),
+                        stop=(a == PASSES - 1),
+                    )
+                nc.scalar.activation(grads[s][:, cols], bank[:], IDENT, scale=-1.0)
+
+        zt = [[kept(f"zt{g}_{c}", [P, 4, BANK], BF16) for c in range(CHUNKS)] for g in range(PASSES)]
+        zcodes = [[kept(f"zcodes{g}_{c}", [P, BANK], U32) for c in range(CHUNKS)] for g in range(PASSES)]
+        zscale = [[kept(f"zscale{g}_{c}", [P, BANK], U8) for c in range(CHUNKS)] for g in range(PASSES)]
+        dcodes = [kept(f"dcodes{g}", [P, N], U32) for g in range(PASSES)]
+        dscale = [kept(f"dscale{g}", [P, N], U8) for g in range(PASSES)]
+        result = [[kept(f"result{c}_{n}", [P, BANK], F32) for n in range(NT)] for c in range(CHUNKS)]
+        olds = {}
+        woven = {}
+
+        def load_old(s):
+            olds[s] = rows.tile([P, T2], F32, name="rowtile", tag="rows", align_bytes=64)
+            nc.sync.dma_start(olds[s][:], old[P * s : P * (s + 1), :])
+
+        def quantise_dec(g):
+            raw = rows.tile([P, 4, N], F32, name="rowtile", tag="rows", align_bytes=64)
+            nc.sync.dma_start(raw[:], dec[BANK * g : BANK * (g + 1), :].rearrange("(p j) n -> p j n", j=4))
+            grouped = weave.tile([P, 4 * N], BF16, name="woven", align_bytes=64)
+            nc.scalar.copy(
+                grouped[:].rearrange("p (c i j) -> p c j i", i=4, j=4),
+                raw[:].rearrange("p j (c i) -> p c j i", i=4),
+            )
+            nc.vector.quantize_mx(out=dcodes[g][:].bitcast(FP8X4), scales=dscale[g][:], in_=grouped[:])
+
+        def scatter(s):
+            page = pages[s % 2]
+            if s == 0:
+                for i in range(2):
+                    cols = slice(BANK * i, BANK * (i + 1))
+                    nc.vector.tensor_tensor(
+                        page[:].indirect(place[:, 32 * i : 32 * i + 32]), grads[s][:, cols], steps[:, cols], MULT
+                    )
+            else:
+                nc.vector.tensor_tensor(page[:].indirect(place[:]), grads[s][:], steps[:], MULT)
+
+        def turn(source, c, first):
+            for j in range(4):
+                t0 = BANK * c + P * j
+                nc.tensor.matmul(
+                    banks[c][:, P * j : P * (j + 1)],
+                    source[:, t0 : t0 + P],
+                    ident[:],
+                    start=(first and j == 0),
+                    stop=(not first and j == 3),
+                    is_transpose=True,
+                )
+
+        def round_rows(s, c):
+            g, b = divmod(s, 4)
+            nc.scalar.copy(
+                zt[g][c][:].rearrange("t j (u b p e) -> t j b u p e", u=2, b=4, e=2)[:, :, b],
+                banks[c][:].rearrange("t (j p u e) -> t j u p e", j=4, u=2, e=2),
+            )
+
+        def turn_back(g, c, half, bank):
+            words = zt[g][c][:].bitcast(F32)
+            for u in range(2):
+                for jj in range(2):
+                    o = 256 * u + P * jj
+                    nc.tensor.transpose(bank[:, o : o + P], words[:, 2 * half + jj, P * u : P * (u + 1)], ident[:])
+
+        def interleave(g, c, half, bank, on_vector):
+            if half == 0:
+                woven[g, c] = weave.tile([P, 4 * BANK], BF16, name="woven", align_bytes=64)
+            dst = woven[g, c][:].bitcast(F32)[:, BANK * half : BANK * (half + 1)].rearrange("p (t u) -> p t u", u=2)
+            src = bank[:].rearrange("p (u t) -> p t u", u=2)
+            if on_vector:
+                nc.vector.tensor_copy(dst, src)
+            else:
+                nc.scalar.copy(dst, src)
+
+        def quantise(g, c):
+            nc.vector.quantize_mx(out=zcodes[g][c][:].bitcast(FP8X4), scales=zscale[g][c][:], in_=woven[g, c][:])
+
+        def decode(g, c, n, bank, start, stop):
+            nc.tensor.matmul_mx(
+                out=bank[:],
+                lhsT=dcodes[g][:, P * n : P * (n + 1)].bitcast(FP8X4),
+                lhsT_scale=dscale[g][:, P * n : P * (n + 1)],
+                rhs=zcodes[g][c][:].bitcast(FP8X4),
+                rhs_scale=zscale[g][c][:],
+                start=start,
+                stop=stop,
+            )
+
+        def with_bias(c, n, bank):
+            nc.scalar.activation(result[c][n][:], bank[:], IDENT, bias=bias[:, n : n + 1])
+
+        def partial(c, n, bank):
+            decode(0, c, n, bank, True, True)
+            with_bias(c, n, bank)
+
+        whole = [(0, 0), (0, 1), (2, 3), (3, 0), (3, 1)]
+        parts = [(c, n) for c in range(CHUNKS) for n in range(NT) if (c, n) not in whole]
+        final_bank = [[6, 7, 0, 1], [2, 3, 6, 7], [0, 1, 2, 3], [6, 7, 0, 1]]
+
+        load_old(0)
+        for s in range(SLICES):
+            if s + 1 < SLICES:
+                load_old(s + 1)
+            for c in range(CHUNKS):
+                turn(olds[s], c, True)
+            if s == SLICES - 1:
+                for n in range(2):
+                    decode(0, 0, n, banks[final_bank[0][n]], True, False)
+            scatter(s)
+            if s == SLICES - 1:
+                break
+            for c in range(CHUNKS):
+                turn(pages[s % 2], c, False)
+                round_rows(s, c)
+            if s in (0, 1):
+                quantise_dec(s)
+            if s == 2:
+                with nc.allow_non_contiguous_dma(reason="one bias value a partition"):
+                    nc.sync.dma_start(bias[:], bd.rearrange("(n p) -> p n", p=P))
+            if s == 3:
+                for c in range(CHUNKS):
+                    for half in range(2):
+                        bank = banks[(2 * c + half) % 4]
+                        turn_back(0, c, half, bank)
+                        interleave(0, c, half, bank, False)
+                    quantise(0, c)
+            if s == 5:
+                for k in range(7):
+                    partial(*parts[k], banks[k])
+            if s == 6:
+                for k in range(7, 11):
+                    partial(*parts[k], banks[k - 7])
+
+        last = SLICES - 1
+
+        def finish(c):
+            for n in range(NT):
+                bank = banks[final_bank[c][n]]
+                if (c, n) in whole:
+                    if c > 0:
+                        decode(0, c, n, bank, True, False)
+                    decode(1, c, n, bank, False, True)
+                    with_bias(c, n, bank)
+                else:
+                    decode(1, c, n, bank, True, True)
+                    nc.vector.tensor_tensor(result[c][n][:], bank[:], result[c][n][:], ADD)
+                nc.sync.dma_start(out[P * n : P * (n + 1), BANK * c : BANK * (c + 1)], result[c][n][:])
+
+        turn(pages[last % 2], 0, False)
+        round_rows(last, 0)
+        for c in range(CHUNKS):
+            if c + 1 < CHUNKS:
+                turn(pages[last % 2], c + 1, False)
+            for half in range(2):
+                turn_back(1, c, half, banks[4 + half])
+                interleave(1, c, half, banks[4 + half], c == 0 and half == 1)
+            if c + 1 < CHUNKS:
+                round_rows(last, c + 1)
+            if c > 0:
+                finish(c - 1)
+            quantise(1, c)
+        finish(CHUNKS - 1)

@@ -24,6 +24,7 @@ PASSES = 2
 SLICES = H // P
 CHUNKS = T2 // BANK
 NT = N // P
+SLOT = (0, 1, 2, 3)
 
 
 def tile_list_sparse_optimiser_step_kernel(
@@ -33,6 +34,7 @@ def tile_list_sparse_optimiser_step_kernel(
     with ExitStack() as ctx:
         keep = ctx.enter_context(tc.tile_pool(name="keep", bufs=1))
         rows = ctx.enter_context(tc.tile_pool(name="rows", bufs=3))
+        reuse = ctx.enter_context(tc.tile_pool(name="reuse", bufs=1))
         weave = ctx.enter_context(tc.tile_pool(name="weave", bufs=4))
         psum = ctx.enter_context(tc.psum_pool(name="psum", bufs=1))
 
@@ -48,10 +50,11 @@ def tile_list_sparse_optimiser_step_kernel(
         vscale = [kept(f"vscale{a}", [P, S], U8) for a in range(PASSES)]
         twords = [
             rows.tile([P, T], U32, name="twords0", tag="rows", align_bytes=64),
-            keep.tile([P, T], U32, name="twords1", tag="late", align_bytes=64),
+            reuse.tile([P, T], U32, name="twords1", align_bytes=64, offset=0),
         ]
         picked = rows.tile([P, S], U8, name="picked", tag="rows", align_bytes=64)
-        wwords = rows.tile([P, PASSES, 2 * H], U8, name="wwords", tag="rows", align_bytes=64)
+        wwords = rows.tile([P, PASSES, H], U8, name="wwords", tag="rows", align_bytes=64)
+        wlate = keep.tile([P, PASSES, H], U8, name="wlate", tag="late", align_bytes=64)
         pages = [kept("page0", [P, T2], F32)]
         ident = kept("ident", [P, P], F32)
         bias = kept("bias", [P, NT], F32)
@@ -75,9 +78,11 @@ def tile_list_sparse_optimiser_step_kernel(
         nc.sync.dma_start(twords[0][:].bitcast(I32), tab_words[0].rearrange("p t i -> p (t i)").bitcast(I32))
         nc.sync.dma_start(place[:], offs2)
         nc.sync.dma_start(twords[1][:].bitcast(I32), tab_words[1].rearrange("p t i -> p (t i)").bitcast(I32))
-        nc.sync.dma_start(wwords[:].bitcast(I32), w4_words.rearrange("a p c -> p a c").bitcast(I32))
+        w4_view = w4_words.rearrange("a p c -> p a c").bitcast(I32)
+        nc.sync.dma_start(wwords[:].bitcast(I32), w4_view[:, :, 0:256])
         steps = kept("steps", [P, S], F32)
         nc.sync.dma_start(steps[:], wgs)
+        nc.sync.dma_start(wlate[:].bitcast(I32), w4_view[:, :, 256:512])
         for q in range(4):
             nc.scalar.dma_start(
                 wscale[32 * q : 32 * q + 4, :, :].bitcast(I32),
@@ -94,18 +99,32 @@ def tile_list_sparse_optimiser_step_kernel(
             for a in range(PASSES):
                 nc.vector.tensor_copy(vwords[a][i], twords[a][:].indirect(pick[:, 32 * i : 32 * i + 32]))
 
+        dealt_words = reuse.tile([P, PASSES, 2 * BANK], U8, name="dealt_words", align_bytes=64, offset=0)
+        dealt_scale = reuse.tile([P, PASSES, BANK], U8, name="dealt_scale", align_bytes=64, offset=2048)
+        nc.vector.tensor_copy(
+            dealt_scale[:].bitcast(I32).rearrange("p a (t g) -> p a t g", t=4),
+            wscale[:].bitcast(I32)[:, :, 128:256].rearrange("p a (g t) -> p a t g", t=4),
+        )
+        nc.vector.tensor_copy(
+            dealt_words[:].bitcast(I32).rearrange("p a (t g w) -> p a t g w", t=4, w=2),
+            wlate[:].bitcast(I32).rearrange("p a (g t w) -> p a t g w", t=4, w=2),
+        )
         pages.append(keep.tile([P, T2], F32, name="page1", tag="late", align_bytes=64))
         nc.gpsimd.memset(pages[1][:], 0.0)
-        grads = [kept(f"grad{s}", [P, S], F32) for s in range(SLICES)]
+        grads = [keep.tile([P, S], F32, name=f"grad{s}", tag=f"grad{s}", align_bytes=64) for s in range(SLICES)]
         for s in range(SLICES):
             for i in range(2):
                 bank = banks[(2 * s + i) % 8]
                 cols = slice(BANK * i, BANK * (i + 1))
+                if s < 4:
+                    w, ws, b = wwords, wscale, s
+                else:
+                    w, ws, b = dealt_words, dealt_scale, SLOT[s - 4]
                 for a in range(PASSES):
                     nc.tensor.matmul_mx(
                         out=bank[:],
-                        lhsT=wwords[:, a, 2 * P * s : 2 * P * (s + 1)].bitcast(FP4X4),
-                        lhsT_scale=wscale[:, a, P * s : P * (s + 1)],
+                        lhsT=w[:, a, 2 * P * b : 2 * P * (b + 1)].bitcast(FP4X4),
+                        lhsT_scale=ws[:, a, P * b : P * (b + 1)],
                         rhs=vwords[a][i].bitcast(FP8X4),
                         rhs_scale=vscale[a][:, cols],
                         start=(a == 0),
@@ -113,7 +132,19 @@ def tile_list_sparse_optimiser_step_kernel(
                     )
                 nc.scalar.activation(grads[s][:, cols], bank[:], IDENT, scale=-1.0)
 
-        zt = [[kept(f"zt{g}_{c}", [P, 4, BANK], BF16) for c in range(CHUNKS)] for g in range(PASSES)]
+        zt = [[kept(f"zt_{c}", [P, 4, BANK], BF16) for c in range(CHUNKS)]]
+        ztw = [kept(f"ztw{c}", [P, 4, P, 2], BF16) for c in range(CHUNKS)]
+        halves = [kept(f"halves{c}", [P, 2, BANK], F32) for c in range(CHUNKS)]
+        factor = {s: steps for s in range(4)}
+
+        def dealt(x, slot):
+            return x.rearrange("(g t i) c -> t g i c", t=4, i=4)[slot]
+
+        def load_factor(s):
+            factor[s] = keep.tile([P, S], F32, name=f"factor{s}", tag=f"grad{s - 4}", align_bytes=64)
+            for m in range(4):
+                nc.sync.dma_start(factor[s][32 * m : 32 * (m + 1), :], dealt(wgs, SLOT[s - 4]))
+
         zcodes = [[kept(f"zcodes{g}_{c}", [P, BANK], U32) for c in range(CHUNKS)] for g in range(PASSES)]
         zscale = [[kept(f"zscale{g}_{c}", [P, BANK], U8) for c in range(CHUNKS)] for g in range(PASSES)]
         dcodes = [kept(f"dcodes{g}", [P, N], U32) for g in range(PASSES)]
@@ -124,11 +155,15 @@ def tile_list_sparse_optimiser_step_kernel(
 
         def load_old(s):
             olds[s] = rows.tile([P, T2], F32, name="rowtile", tag="rows", align_bytes=64)
-            nc.sync.dma_start(olds[s][:], old[P * s : P * (s + 1), :])
+            nc.sync.dma_start(olds[s][:], old[P * s : P * (s + 1), :] if s < 4 else dealt(old[BANK:, :], SLOT[s - 4]))
 
         def quantise_dec(g):
             raw = rows.tile([P, 4, N], F32, name="rowtile", tag="rows", align_bytes=64)
-            nc.sync.dma_start(raw[:], dec[BANK * g : BANK * (g + 1), :].rearrange("(p j) n -> p j n", j=4))
+            if g == 0:
+                nc.sync.dma_start(raw[:], dec[:BANK, :].rearrange("(p j) n -> p j n", j=4))
+            else:
+                for slot in range(4):
+                    nc.sync.dma_start(raw[:, slot, :], dealt(dec[BANK:, :], slot))
             grouped = weave.tile([P, 4 * N], BF16, name="woven", align_bytes=64)
             nc.scalar.copy(
                 grouped[:].rearrange("p (c i j) -> p c j i", i=4, j=4),
@@ -145,7 +180,7 @@ def tile_list_sparse_optimiser_step_kernel(
                         page[:].indirect(place[:, 32 * i : 32 * i + 32]), grads[s][:, cols], steps[:, cols], MULT
                     )
             else:
-                nc.vector.tensor_tensor(page[:].indirect(place[:]), grads[s][:], steps[:], MULT)
+                nc.vector.tensor_tensor(page[:].indirect(place[:]), grads[s][:], factor[s][:], MULT)
 
         def turn(source, c, first):
             for j in range(4):
@@ -200,29 +235,40 @@ def tile_list_sparse_optimiser_step_kernel(
         def with_bias(c, n, bank):
             nc.scalar.activation(result[c][n][:], bank[:], IDENT, bias=bias[:, n : n + 1])
 
-        def partial(c, n, bank):
-            decode(0, c, n, bank, True, True)
-            with_bias(c, n, bank)
+        def second_half(c):
+            return halves[c][:, 1, :].bitcast(BF16).rearrange("p (t e) -> p t e", e=2)
 
-        whole = [(0, 0), (0, 1), (2, 3), (3, 0), (3, 1)]
-        parts = [(c, n) for c in range(CHUNKS) for n in range(NT) if (c, n) not in whole]
-        final_bank = [[6, 7, 0, 1], [2, 3, 6, 7], [0, 1, 2, 3], [6, 7, 0, 1]]
+        def back(source, c):
+            for j in range(4):
+                nc.tensor.transpose(banks[4 + c][:, P * j : P * (j + 1)], source[:, j, :], ident[:])
 
+        def open_chunk(c):
+            for n in range(NT):
+                decode(0, c, n, banks[(4 * c + n) % 8], True, False)
+
+        last = SLICES - 1
         load_old(0)
-        for s in range(SLICES):
-            if s + 1 < SLICES:
-                load_old(s + 1)
+        for s in range(last):
+            load_old(s + 1)
             for c in range(CHUNKS):
                 turn(olds[s], c, True)
-            if s == SLICES - 1:
-                for n in range(2):
-                    decode(0, 0, n, banks[final_bank[0][n]], True, False)
             scatter(s)
-            if s == SLICES - 1:
-                break
+            if s < 4:
+                load_factor(s + 4)
             for c in range(CHUNKS):
                 turn(pages[s % 2], c, False)
-                round_rows(s, c)
+                if s < 4:
+                    round_rows(s, c)
+                elif s == 6:
+                    turned = weave.tile([P, 4, P], F32, name="turned", tag="turned", bufs=2)
+                    nc.scalar.copy(turned[:].rearrange("t j p -> t (j p)"), banks[c][:])
+                    back(turned, c)
+                    nc.scalar.copy(second_half(c), banks[4 + c][:].unsqueeze(2).to_broadcast([P, BANK, 2]))
+                else:
+                    nc.scalar.copy(ztw[c][:, :, :, s - 4], banks[c][:].rearrange("t (j p) -> t j p", j=4))
+                    if s == 5:
+                        back(ztw[c][:].rearrange("t j p e -> t j (p e)").bitcast(F32), c)
+                        nc.scalar.copy(halves[c][:, 0, :], banks[4 + c][:])
             if s in (0, 1):
                 quantise_dec(s)
             if s == 2:
@@ -231,43 +277,29 @@ def tile_list_sparse_optimiser_step_kernel(
             if s == 3:
                 for c in range(CHUNKS):
                     for half in range(2):
-                        bank = banks[(2 * c + half) % 4]
+                        bank = banks[4 + (2 * c + half) % 4]
                         turn_back(0, c, half, bank)
                         interleave(0, c, half, bank, False)
                     quantise(0, c)
-            if s == 5:
-                for k in range(7):
-                    partial(*parts[k], banks[k])
-            if s == 6:
-                for k in range(7, 11):
-                    partial(*parts[k], banks[k - 7])
+        open_chunk(0)
+        open_chunk(1)
+        scatter(last)
 
-        last = SLICES - 1
-
-        def finish(c):
-            for n in range(NT):
-                bank = banks[final_bank[c][n]]
-                if (c, n) in whole:
-                    if c > 0:
-                        decode(0, c, n, bank, True, False)
-                    decode(1, c, n, bank, False, True)
-                    with_bias(c, n, bank)
-                else:
-                    decode(1, c, n, bank, True, True)
-                    nc.vector.tensor_tensor(result[c][n][:], bank[:], result[c][n][:], ADD)
-                nc.sync.dma_start(out[P * n : P * (n + 1), BANK * c : BANK * (c + 1)], result[c][n][:])
-
-        turn(pages[last % 2], 0, False)
-        round_rows(last, 0)
         for c in range(CHUNKS):
-            if c + 1 < CHUNKS:
-                turn(pages[last % 2], c + 1, False)
-            for half in range(2):
-                turn_back(1, c, half, banks[4 + half])
-                interleave(1, c, half, banks[4 + half], c == 0 and half == 1)
-            if c + 1 < CHUNKS:
-                round_rows(last, c + 1)
-            if c > 0:
-                finish(c - 1)
+            cols = slice(BANK * c, BANK * (c + 1))
+            nc.vector.tensor_tensor(second_half(c)[:, :, 1], olds[last][:, cols], pages[last % 2][:, cols], ADD)
+            woven[1, c] = weave.tile([P, 4 * BANK], BF16, name="woven", align_bytes=64)
+            nc.vector.tensor_copy(
+                woven[1, c][:].bitcast(F32).rearrange("p (t u) -> p t u", u=2), halves[c][:].rearrange("p u t -> p t u")
+            )
             quantise(1, c)
-        finish(CHUNKS - 1)
+            for n in range(NT):
+                bank = banks[(4 * c + n) % 8]
+                decode(1, c, n, bank, False, True)
+                if c == CHUNKS - 1 and n % 2 == 1:
+                    nc.vector.tensor_scalar_add(result[c][n][:], bank[:], bias[:, n : n + 1])
+                else:
+                    with_bias(c, n, bank)
+                nc.sync.dma_start(out[P * n : P * (n + 1), cols], result[c][n][:])
+            if c + 2 < CHUNKS:
+                open_chunk(c + 2)

@@ -110,7 +110,7 @@ def tile_list_sparse_optimiser_step_kernel(
             wlate[:].bitcast(I32).rearrange("p a (g t w) -> p a t g w", t=4, w=2),
         )
         pages.append(keep.tile([P, T2], F32, name="page1", tag="late", align_bytes=64))
-        nc.gpsimd.memset(pages[1][:], 0.0)
+        nc.vector.memset(pages[1][:], 0.0)
         grads = [keep.tile([P, S], F32, name=f"grad{s}", tag=f"grad{s}", align_bytes=64) for s in range(SLICES)]
         for s in range(SLICES):
             for i in range(2):
@@ -135,15 +135,18 @@ def tile_list_sparse_optimiser_step_kernel(
         zt = [[kept(f"zt_{c}", [P, 4, BANK], BF16) for c in range(CHUNKS)]]
         ztw = [kept(f"ztw{c}", [P, 4, P, 2], BF16) for c in range(CHUNKS)]
         halves = [kept(f"halves{c}", [P, 2, BANK], F32) for c in range(CHUNKS)]
-        factor = {s: steps for s in range(4)}
+        turned = [kept(f"turned{c}", [P, 4, P], F32) for c in range(CHUNKS)]
+        factor = {s: steps[:] for s in range(4)}
 
         def dealt(x, slot):
             return x.rearrange("(g t i) c -> t g i c", t=4, i=4)[slot]
 
+        factors = reuse.tile([P, 4, S], F32, name="factors", align_bytes=64, offset=4096)
+
         def load_factor(s):
-            factor[s] = keep.tile([P, S], F32, name=f"factor{s}", tag=f"grad{s - 4}", align_bytes=64)
+            factor[s] = factors[:, s - 4, :]
             for m in range(4):
-                nc.sync.dma_start(factor[s][32 * m : 32 * (m + 1), :], dealt(wgs, SLOT[s - 4]))
+                nc.sync.dma_start(factors[32 * m : 32 * (m + 1), s - 4, :], dealt(wgs, SLOT[s - 4]))
 
         zcodes = [[kept(f"zcodes{g}_{c}", [P, BANK], U32) for c in range(CHUNKS)] for g in range(PASSES)]
         zscale = [[kept(f"zscale{g}_{c}", [P, BANK], U8) for c in range(CHUNKS)] for g in range(PASSES)]
@@ -180,7 +183,7 @@ def tile_list_sparse_optimiser_step_kernel(
                         page[:].indirect(place[:, 32 * i : 32 * i + 32]), grads[s][:, cols], steps[:, cols], MULT
                     )
             else:
-                nc.vector.tensor_tensor(page[:].indirect(place[:]), grads[s][:], factor[s][:], MULT)
+                nc.vector.tensor_tensor(page[:].indirect(place[:]), grads[s][:], factor[s], MULT)
 
         def turn(source, c, first):
             for j in range(4):
@@ -221,13 +224,13 @@ def tile_list_sparse_optimiser_step_kernel(
         def quantise(g, c):
             nc.vector.quantize_mx(out=zcodes[g][c][:].bitcast(FP8X4), scales=zscale[g][c][:], in_=woven[g, c][:])
 
-        def decode(g, c, n, bank, start, stop):
+        def decode(g, c, n, acc, start, stop, cols=slice(0, BANK)):
             nc.tensor.matmul_mx(
-                out=bank[:],
+                out=acc,
                 lhsT=dcodes[g][:, P * n : P * (n + 1)].bitcast(FP8X4),
                 lhsT_scale=dscale[g][:, P * n : P * (n + 1)],
-                rhs=zcodes[g][c][:].bitcast(FP8X4),
-                rhs_scale=zscale[g][c][:],
+                rhs=zcodes[g][c][:, cols].bitcast(FP8X4),
+                rhs_scale=zscale[g][c][:, cols],
                 start=start,
                 stop=stop,
             )
@@ -244,7 +247,13 @@ def tile_list_sparse_optimiser_step_kernel(
 
         def open_chunk(c):
             for n in range(NT):
-                decode(0, c, n, banks[(4 * c + n) % 8], True, False)
+                decode(0, c, n, banks[(4 * c + n) % 8][:], True, False)
+
+        def narrow(g, half):
+            for n in range(NT):
+                acc = banks[2 * half + n // 2][:, 256 * (n % 2) : 256 * (n % 2 + 1)]
+                cols = slice(256 * half, 256 * (half + 1))
+                decode(g, 0, n, acc, g == 0 and n % 2 == 0, g == 1 and n % 2 == 1, cols)
 
         last = SLICES - 1
         load_old(0)
@@ -260,15 +269,16 @@ def tile_list_sparse_optimiser_step_kernel(
                 if s < 4:
                     round_rows(s, c)
                 elif s == 6:
-                    turned = weave.tile([P, 4, P], F32, name="turned", tag="turned", bufs=2)
-                    nc.scalar.copy(turned[:].rearrange("t j p -> t (j p)"), banks[c][:])
-                    back(turned, c)
-                    nc.scalar.copy(second_half(c), banks[4 + c][:].unsqueeze(2).to_broadcast([P, BANK, 2]))
+                    nc.scalar.copy(turned[c][:].rearrange("t j p -> t (j p)"), banks[c][:])
                 else:
                     nc.scalar.copy(ztw[c][:, :, :, s - 4], banks[c][:].rearrange("t (j p) -> t j p", j=4))
                     if s == 5:
                         back(ztw[c][:].rearrange("t j p e -> t j (p e)").bitcast(F32), c)
                         nc.scalar.copy(halves[c][:, 0, :], banks[4 + c][:])
+            if s == 6:
+                for c in range(CHUNKS):
+                    back(turned[c], c)
+                    nc.scalar.copy(second_half(c), banks[4 + c][:].unsqueeze(2).to_broadcast([P, BANK, 2]))
             if s in (0, 1):
                 quantise_dec(s)
             if s == 2:
@@ -281,21 +291,41 @@ def tile_list_sparse_optimiser_step_kernel(
                         turn_back(0, c, half, bank)
                         interleave(0, c, half, bank, False)
                     quantise(0, c)
-        open_chunk(0)
+        narrow(0, 0)
+        narrow(0, 1)
         open_chunk(1)
         scatter(last)
 
-        for c in range(CHUNKS):
-            cols = slice(BANK * c, BANK * (c + 1))
-            nc.vector.tensor_tensor(second_half(c)[:, :, 1], olds[last][:, cols], pages[last % 2][:, cols], ADD)
-            woven[1, c] = weave.tile([P, 4 * BANK], BF16, name="woven", align_bytes=64)
+        def finish_rows(c, lo, hi):
+            cols = slice(BANK * c + lo, BANK * c + hi)
+            nc.vector.tensor_tensor(second_half(c)[:, lo:hi, 1], olds[last][:, cols], pages[last % 2][:, cols], ADD)
+            ready = weave.tile([P, 4 * (hi - lo)], BF16, name="ready", tag="woven", align_bytes=64)
             nc.vector.tensor_copy(
-                woven[1, c][:].bitcast(F32).rearrange("p (t u) -> p t u", u=2), halves[c][:].rearrange("p u t -> p t u")
+                ready[:].bitcast(F32).rearrange("p (t u) -> p t u", u=2),
+                halves[c][:, :, lo:hi].rearrange("p u t -> p t u"),
             )
-            quantise(1, c)
+            nc.vector.quantize_mx(out=zcodes[1][c][:, lo:hi].bitcast(FP8X4), scales=zscale[1][c][:, lo:hi], in_=ready[:])
+
+        for half in range(2):
+            finish_rows(0, 256 * half, 256 * (half + 1))
+            narrow(1, half)
+            for pair in range(2):
+                staged = result[0][2 * half + pair]
+                for k in range(2):
+                    n = 2 * pair + k
+                    cols = slice(256 * k, 256 * (k + 1))
+                    nc.scalar.activation(staged[:, cols], banks[2 * half + pair][:, cols], IDENT, bias=bias[:, n : n + 1])
+                nc.sync.dma_start(
+                    out[2 * P * pair : 2 * P * (pair + 1), 256 * half : 256 * (half + 1)].rearrange("(k p) t -> p k t", p=P),
+                    staged[:].rearrange("p (k t) -> p k t", k=2),
+                )
+        open_chunk(2)
+        for c in range(1, CHUNKS):
+            cols = slice(BANK * c, BANK * (c + 1))
+            finish_rows(c, 0, BANK)
             for n in range(NT):
                 bank = banks[(4 * c + n) % 8]
-                decode(1, c, n, bank, False, True)
+                decode(1, c, n, bank[:], False, True)
                 if c == CHUNKS - 1 and n % 2 == 1:
                     nc.vector.tensor_scalar_add(result[c][n][:], bank[:], bias[:, n : n + 1])
                 else:

@@ -50,18 +50,14 @@ def tile_list_sparse_optimiser_step_kernel(
         vscale = [kept(f"vscale{a}", [P, S], U8) for a in range(PASSES)]
         twords = [
             rows.tile([P, T], U32, name="twords0", tag="rows", align_bytes=64),
-            reuse.tile([P, T], U32, name="twords1", align_bytes=64, offset=0),
+            reuse.tile([P, T], U32, name="twords1", align_bytes=64, offset=7168),
         ]
         picked = rows.tile([P, S], U8, name="picked", tag="rows", align_bytes=64)
-        wwords = rows.tile([P, PASSES, H], U8, name="wwords", tag="rows", align_bytes=64)
-        wlate = keep.tile([P, PASSES, H], U8, name="wlate", tag="late", align_bytes=64)
+        wwords = rows.tile([P, PASSES, 2 * H], U8, name="wwords", tag="rows", align_bytes=64)
         pages = [kept("page0", [P, T2], F32)]
         ident = kept("ident", [P, P], F32)
         bias = kept("bias", [P, NT], F32)
-        warm = kept("warm", [P, 16], F32)
 
-        nc.gpsimd.memset(warm[:], 0.0)
-        nc.scalar.activation(warm[:, 8:9], warm[:, 0:1], IDENT, scale=-1.0)
         for q in range(4):
             nc.vector.memset(tscale[32 * q : 32 * q + 24, :].bitcast(I32), 0)
         nc.gpsimd.memset(wscale[:].rearrange("p a c -> p (a c)").bitcast(I32), 0)
@@ -78,11 +74,9 @@ def tile_list_sparse_optimiser_step_kernel(
         nc.sync.dma_start(twords[0][:].bitcast(I32), tab_words[0].rearrange("p t i -> p (t i)").bitcast(I32))
         nc.sync.dma_start(place[:], offs2)
         nc.sync.dma_start(twords[1][:].bitcast(I32), tab_words[1].rearrange("p t i -> p (t i)").bitcast(I32))
-        w4_view = w4_words.rearrange("a p c -> p a c").bitcast(I32)
-        nc.sync.dma_start(wwords[:].bitcast(I32), w4_view[:, :, 0:256])
+        nc.sync.dma_start(wwords[:].bitcast(I32), w4_words.rearrange("a p c -> p a c").bitcast(I32))
         steps = kept("steps", [P, S], F32)
         nc.sync.dma_start(steps[:], wgs)
-        nc.sync.dma_start(wlate[:].bitcast(I32), w4_view[:, :, 256:512])
         for q in range(4):
             nc.scalar.dma_start(
                 wscale[32 * q : 32 * q + 4, :, :].bitcast(I32),
@@ -95,21 +89,21 @@ def tile_list_sparse_optimiser_step_kernel(
         for a in range(PASSES):
             first = 24 + 4 * a
             nc.scalar.dma_start(vscale[a][0:100, :].bitcast(I32), picked[first : first + 100, :].bitcast(I32))
-        for i in range(2):
-            for a in range(PASSES):
+        for a in range(PASSES):
+            for i in range(2):
                 nc.vector.tensor_copy(vwords[a][i], twords[a][:].indirect(pick[:, 32 * i : 32 * i + 32]))
 
-        dealt_words = reuse.tile([P, PASSES, 2 * BANK], U8, name="dealt_words", align_bytes=64, offset=0)
-        dealt_scale = reuse.tile([P, PASSES, BANK], U8, name="dealt_scale", align_bytes=64, offset=2048)
+        dealt_words = reuse.tile([P, PASSES, 2 * BANK], U8, name="dealt_words", align_bytes=64, offset=8192)
+        dealt_scale = reuse.tile([P, PASSES, BANK], U8, name="dealt_scale", align_bytes=64, offset=10240)
         nc.vector.tensor_copy(
             dealt_scale[:].bitcast(I32).rearrange("p a (t g) -> p a t g", t=4),
             wscale[:].bitcast(I32)[:, :, 128:256].rearrange("p a (g t) -> p a t g", t=4),
         )
         nc.vector.tensor_copy(
             dealt_words[:].bitcast(I32).rearrange("p a (t g w) -> p a t g w", t=4, w=2),
-            wlate[:].bitcast(I32).rearrange("p a (g t w) -> p a t g w", t=4, w=2),
+            wwords[:].bitcast(I32)[:, :, 256:512].rearrange("p a (g t w) -> p a t g w", t=4, w=2),
         )
-        pages.append(keep.tile([P, T2], F32, name="page1", tag="late", align_bytes=64))
+        pages.append(reuse.tile([P, T2], F32, name="page1", align_bytes=64, offset=0))
         nc.vector.memset(pages[1][:], 0.0)
         grads = [keep.tile([P, S], F32, name=f"grad{s}", tag=f"grad{s}", align_bytes=64) for s in range(SLICES)]
         for s in range(SLICES):
@@ -141,7 +135,7 @@ def tile_list_sparse_optimiser_step_kernel(
         def dealt(x, slot):
             return x.rearrange("(g t i) c -> t g i c", t=4, i=4)[slot]
 
-        factors = reuse.tile([P, 4, S], F32, name="factors", align_bytes=64, offset=4096)
+        factors = reuse.tile([P, 4, S], F32, name="factors", align_bytes=64, offset=12288)
 
         def load_factor(s):
             factor[s] = factors[:, s - 4, :]
@@ -175,15 +169,7 @@ def tile_list_sparse_optimiser_step_kernel(
             nc.vector.quantize_mx(out=dcodes[g][:].bitcast(FP8X4), scales=dscale[g][:], in_=grouped[:])
 
         def scatter(s):
-            page = pages[s % 2]
-            if s == 0:
-                for i in range(2):
-                    cols = slice(BANK * i, BANK * (i + 1))
-                    nc.vector.tensor_tensor(
-                        page[:].indirect(place[:, 32 * i : 32 * i + 32]), grads[s][:, cols], steps[:, cols], MULT
-                    )
-            else:
-                nc.vector.tensor_tensor(page[:].indirect(place[:]), grads[s][:], factor[s], MULT)
+            nc.vector.tensor_tensor(pages[s % 2][:].indirect(place[:]), grads[s][:], factor[s], MULT)
 
         def turn(source, c, first):
             for j in range(4):
@@ -245,15 +231,20 @@ def tile_list_sparse_optimiser_step_kernel(
             for j in range(4):
                 nc.tensor.transpose(banks[4 + c][:, P * j : P * (j + 1)], source[:, j, :], ident[:])
 
-        def open_chunk(c):
-            for n in range(NT):
-                decode(0, c, n, banks[(4 * c + n) % 8][:], True, False)
+        units = [(0, 0, 256), (0, 256, 512), (1, 0, 512), (2, 0, 512), (3, 0, 256), (3, 256, 512)]
 
-        def narrow(g, half):
-            for n in range(NT):
-                acc = banks[2 * half + n // 2][:, 256 * (n % 2) : 256 * (n % 2 + 1)]
-                cols = slice(256 * half, 256 * (half + 1))
-                decode(g, 0, n, acc, g == 0 and n % 2 == 0, g == 1 and n % 2 == 1, cols)
+        def sums(unit):
+            c, lo, hi = unit
+            width = hi - lo
+            share = BANK // width
+            first = 4 * (c % 2) + 4 * lo // BANK
+            return [banks[first + n // share][:, width * (n % share) : width * (n % share + 1)] for n in range(NT)]
+
+        def multiply(g, unit):
+            c, lo, hi = unit
+            share = BANK // (hi - lo)
+            for n, acc in enumerate(sums(unit)):
+                decode(g, c, n, acc, g == 0 and n % share == 0, g == 1 and n % share == share - 1, slice(lo, hi))
 
         last = SLICES - 1
         load_old(0)
@@ -287,49 +278,64 @@ def tile_list_sparse_optimiser_step_kernel(
             if s == 3:
                 for c in range(CHUNKS):
                     for half in range(2):
-                        bank = banks[4 + (2 * c + half) % 4]
+                        bank = banks[(4 + 2 * c + half) % 8]
                         turn_back(0, c, half, bank)
                         interleave(0, c, half, bank, False)
                     quantise(0, c)
-        narrow(0, 0)
-        narrow(0, 1)
-        open_chunk(1)
+        for unit in units[:3]:
+            multiply(0, unit)
         scatter(last)
 
-        def finish_rows(c, lo, hi):
+        ready = {}
+
+        def subtract(unit):
+            c, lo, hi = unit
             cols = slice(BANK * c + lo, BANK * c + hi)
             nc.vector.tensor_tensor(second_half(c)[:, lo:hi, 1], olds[last][:, cols], pages[last % 2][:, cols], ADD)
-            ready = weave.tile([P, 4 * (hi - lo)], BF16, name="ready", tag="woven", align_bytes=64)
+
+        def join(unit):
+            c, lo, hi = unit
+            ready[unit] = weave.tile([P, 4 * (hi - lo)], BF16, name="ready", tag="woven", align_bytes=64)
             nc.vector.tensor_copy(
-                ready[:].bitcast(F32).rearrange("p (t u) -> p t u", u=2),
+                ready[unit][:].bitcast(F32).rearrange("p (t u) -> p t u", u=2),
                 halves[c][:, :, lo:hi].rearrange("p u t -> p t u"),
             )
-            nc.vector.quantize_mx(out=zcodes[1][c][:, lo:hi].bitcast(FP8X4), scales=zscale[1][c][:, lo:hi], in_=ready[:])
 
-        for half in range(2):
-            finish_rows(0, 256 * half, 256 * (half + 1))
-            narrow(1, half)
-            for pair in range(2):
-                staged = result[0][2 * half + pair]
-                for k in range(2):
-                    n = 2 * pair + k
-                    cols = slice(256 * k, 256 * (k + 1))
-                    nc.scalar.activation(staged[:, cols], banks[2 * half + pair][:, cols], IDENT, bias=bias[:, n : n + 1])
-                nc.sync.dma_start(
-                    out[2 * P * pair : 2 * P * (pair + 1), 256 * half : 256 * (half + 1)].rearrange("(k p) t -> p k t", p=P),
-                    staged[:].rearrange("p (k t) -> p k t", k=2),
-                )
-        open_chunk(2)
-        for c in range(1, CHUNKS):
-            cols = slice(BANK * c, BANK * (c + 1))
-            finish_rows(c, 0, BANK)
-            for n in range(NT):
-                bank = banks[(4 * c + n) % 8]
-                decode(1, c, n, bank[:], False, True)
-                if c == CHUNKS - 1 and n % 2 == 1:
-                    nc.vector.tensor_scalar_add(result[c][n][:], bank[:], bias[:, n : n + 1])
+        def finish(unit):
+            c, lo, hi = unit
+            width = hi - lo
+            share = BANK // width
+            nc.vector.quantize_mx(
+                out=zcodes[1][c][:, lo:hi].bitcast(FP8X4), scales=zscale[1][c][:, lo:hi], in_=ready[unit][:]
+            )
+            multiply(1, unit)
+            for n, acc in enumerate(sums(unit)):
+                staged = result[c][4 * lo // BANK + n // share]
+                part = staged[:, width * (n % share) : width * (n % share + 1)]
+                if c == CHUNKS - 1 and n >= 2:
+                    nc.vector.tensor_scalar_add(part, acc, bias[:, n : n + 1])
                 else:
-                    with_bias(c, n, bank)
-                nc.sync.dma_start(out[P * n : P * (n + 1), cols], result[c][n][:])
-            if c + 2 < CHUNKS:
-                open_chunk(c + 2)
+                    nc.scalar.activation(part, acc, IDENT, bias=bias[:, n : n + 1])
+                if n % share == share - 1:
+                    nc.sync.dma_start(
+                        out[P * (n + 1 - share) : P * (n + 1), BANK * c + lo : BANK * c + hi].rearrange(
+                            "(k p) t -> p k t", p=P
+                        ),
+                        staged[:].rearrange("p (k t) -> p k t", k=share),
+                    )
+            if hi == BANK:
+                for later in units:
+                    if later[0] == c + 2:
+                        multiply(0, later)
+
+        subtract(units[0])
+        subtract(units[1])
+        join(units[0])
+        join(units[1])
+        finish(units[0])
+        for i in range(1, len(units)):
+            if i + 1 < len(units):
+                subtract(units[i + 1])
+            finish(units[i])
+            if i + 1 < len(units):
+                join(units[i + 1])

@@ -105,26 +105,30 @@ def tile_list_sparse_optimiser_step_kernel(
         )
         pages.append(reuse.tile([P, T2], F32, name="page1", align_bytes=64, offset=0))
         nc.vector.memset(pages[1][:], 0.0)
-        grads = [keep.tile([P, S], F32, name=f"grad{s}", tag=f"grad{s}", align_bytes=64) for s in range(SLICES)]
-        for s in range(SLICES):
-            for i in range(2):
-                bank = banks[(2 * s + i) % 8]
-                cols = slice(BANK * i, BANK * (i + 1))
-                if s < 4:
-                    w, ws, b = wwords, wscale, s
-                else:
-                    w, ws, b = dealt_words, dealt_scale, SLOT[s - 4]
+        grads = {}
+
+        def expand(s, pair):
+            if s < 4:
+                w, ws, b = wwords, wscale, s
+            else:
+                w, ws, b = dealt_words, dealt_scale, SLOT[s - 4]
+            grads[s] = weave.tile([P, S], F32, name="grad", tag="grad", bufs=4, align_bytes=64)
+            for i, bank in enumerate(pair):
                 for a in range(PASSES):
                     nc.tensor.matmul_mx(
                         out=bank[:],
                         lhsT=w[:, a, 2 * P * b : 2 * P * (b + 1)].bitcast(FP4X4),
                         lhsT_scale=ws[:, a, P * b : P * (b + 1)],
                         rhs=vwords[a][i].bitcast(FP8X4),
-                        rhs_scale=vscale[a][:, cols],
+                        rhs_scale=vscale[a][:, BANK * i : BANK * (i + 1)],
                         start=(a == 0),
                         stop=(a == PASSES - 1),
                     )
-                nc.scalar.activation(grads[s][:, cols], bank[:], IDENT, scale=-1.0)
+                nc.scalar.activation(grads[s][:, BANK * i : BANK * (i + 1)], bank[:], IDENT, scale=-1.0)
+
+        expand(0, banks[0:2])
+        expand(1, banks[2:4])
+        expand(2, banks[4:6])
 
         zt = [[kept(f"zt_{c}", [P, 4, BANK], BF16) for c in range(CHUNKS)]]
         ztw = [kept(f"ztw{c}", [P, 4, P, 2], BF16) for c in range(CHUNKS)]
@@ -263,9 +267,13 @@ def tile_list_sparse_optimiser_step_kernel(
                     nc.scalar.copy(turned[c][:].rearrange("t j p -> t (j p)"), banks[c][:])
                 else:
                     nc.scalar.copy(ztw[c][:, :, :, s - 4], banks[c][:].rearrange("t (j p) -> t j p", j=4))
-                    if s == 5:
-                        back(ztw[c][:].rearrange("t j p e -> t j (p e)").bitcast(F32), c)
-                        nc.scalar.copy(halves[c][:, 0, :], banks[4 + c][:])
+            if s < 4:
+                expand(s + 3, banks[2:4])
+            if s == 5:
+                expand(last, banks[2:4])
+                for c in range(CHUNKS):
+                    back(ztw[c][:].rearrange("t j p e -> t j (p e)").bitcast(F32), c)
+                    nc.scalar.copy(halves[c][:, 0, :], banks[4 + c][:])
             if s == 6:
                 for c in range(CHUNKS):
                     back(turned[c], c)

from contextlib import ExitStack

import concourse.mybir as mybir
from concourse.masks import make_identity

K, T, S, H, T2, N = 1024, 2048, 1024, 1024, 2048, 512
FLOPS = 2 * K * H * S + 2 * H * N * T2

F32 = mybir.dt.float32
BF16 = mybir.dt.bfloat16
I32 = mybir.dt.int32
U32 = mybir.dt.uint32
U16 = mybir.dt.uint16
U8 = mybir.dt.uint8
FP8X4 = mybir.dt.float8_e4m3fn_x4
FP4X4 = mybir.dt.float4_e2m1fn_x4
MULT = mybir.AluOpType.mult
ADD = mybir.AluOpType.add
IDENT = mybir.ActivationFunctionType.Identity

P = 128
BANK = 512
PASSES = 2
SLICES = H // P
CHUNKS = T2 // BANK
NT = N // P
SLOT = (0, 1, 2, 3)


def tile_list_sparse_optimiser_step_kernel(
    tc, tab_words, tab_scales, offs, w4_words, w4_scales, wgs, offs2, old, dec, bd, out
):
    nc = tc.nc
    with ExitStack() as ctx:
        keep = ctx.enter_context(tc.tile_pool(name="keep", bufs=1))
        rows = ctx.enter_context(tc.tile_pool(name="rows", bufs=3))
        reuse = ctx.enter_context(tc.tile_pool(name="reuse", bufs=1))
        weave = ctx.enter_context(tc.tile_pool(name="weave", bufs=4))
        psum = ctx.enter_context(tc.psum_pool(name="psum", bufs=1))

        def kept(name, shape, dtype):
            return keep.tile(shape, dtype, name=name, align_bytes=64)

        banks = [psum.tile([P, BANK], F32, name=f"bank{b}") for b in range(8)]

        pick = keep.tile([P, S // 16], U16, name="pick")
        place = keep.tile([P, S // 16], U16, name="place")
        tscale = keep.tile([P, T], U8, name="tscale", tag="early", align_bytes=64)
        wscale = kept("wscale", [P, PASSES, H], U8)
        vscale = [kept(f"vscale{a}", [P, S], U8) for a in range(PASSES)]
        twords = [
            rows.tile([P, T], U32, name="twords0", tag="rows", align_bytes=64),
            reuse.tile([P, T], U32, name="twords1", align_bytes=64, offset=7168),
        ]
        picked = rows.tile([P, S], U8, name="picked", tag="rows", align_bytes=64)
        wwords = rows.tile([P, PASSES, 2 * H], U8, name="wwords", tag="rows", align_bytes=64)
        pages = [kept("page0", [P, T2], F32)]
        ident = kept("ident", [P, P], F32)
        bias = kept("bias", [P, NT], F32)

        for q in range(4):
            nc.vector.memset(tscale[32 * q : 32 * q + 24, :].bitcast(I32), 0)
        nc.gpsimd.memset(wscale[:].rearrange("p a c -> p (a c)").bitcast(I32), 0)
        for a in range(PASSES):
            nc.gpsimd.memset(vscale[a][96:128, :].bitcast(I32), 0)
        nc.vector.memset(pages[0][:], 0.0)
        make_identity(nc, ident[:])

        nc.sync.dma_start(pick[:], offs)
        for q in range(4):
            nc.sync.dma_start(
                tscale[32 * q + 24 : 32 * q + 32, :].bitcast(I32), tab_scales[:, 4 * q : 4 * q + 4, :].bitcast(I32)
            )
        nc.sync.dma_start(twords[0][:].bitcast(I32), tab_words[0].rearrange("p t i -> p (t i)").bitcast(I32))
        nc.sync.dma_start(place[:], offs2)
        nc.sync.dma_start(twords[1][:].bitcast(I32), tab_words[1].rearrange("p t i -> p (t i)").bitcast(I32))
        nc.sync.dma_start(wwords[:].bitcast(I32), w4_words.rearrange("a p c -> p a c").bitcast(I32))
        steps = kept("steps", [P, S], F32)
        nc.sync.dma_start(steps[:], wgs)
        for q in range(4):
            nc.scalar.dma_start(
                wscale[32 * q : 32 * q + 4, :, :].bitcast(I32),
                w4_scales[:, 4 * q : 4 * q + 4, :].rearrange("a r c -> r a c").bitcast(I32),
            )

        nc.vector.tensor_copy(picked[:], tscale[:].indirect(pick[:]))
        vall = keep.tile([P, PASSES * S], U32, name="vwords", tag="early", align_bytes=64)
        vwords = [[vall[:, S * a + BANK * i : S * a + BANK * (i + 1)] for i in range(2)] for a in range(PASSES)]
        for a in range(PASSES):
            first = 24 + 4 * a
            nc.scalar.dma_start(vscale[a][0:100, :].bitcast(I32), picked[first : first + 100, :].bitcast(I32))
        for a in range(PASSES):
            for i in range(2):
                nc.vector.tensor_copy(vwords[a][i], twords[a][:].indirect(pick[:, 32 * i : 32 * i + 32]))

        dealt_words = reuse.tile([P, PASSES, 2 * BANK], U8, name="dealt_words", align_bytes=64, offset=8192)
        dealt_scale = reuse.tile([P, PASSES, BANK], U8, name="dealt_scale", align_bytes=64, offset=10240)
        nc.vector.tensor_copy(
            dealt_scale[:].bitcast(I32).rearrange("p a (t g) -> p a t g", t=4),
            wscale[:].bitcast(I32)[:, :, 128:256].rearrange("p a (g t) -> p a t g", t=4),
        )
        nc.vector.tensor_copy(
            dealt_words[:].bitcast(I32).rearrange("p a (t g w) -> p a t g w", t=4, w=2),
            wwords[:].bitcast(I32)[:, :, 256:512].rearrange("p a (g t w) -> p a t g w", t=4, w=2),
        )
        pages.append(reuse.tile([P, T2], F32, name="page1", align_bytes=64, offset=0))
        nc.vector.memset(pages[1][:], 0.0)
        grads = {}

        def expand(s, pair):
            if s < 4:
                w, ws, b = wwords, wscale, s
            else:
                w, ws, b = dealt_words, dealt_scale, SLOT[s - 4]
            grads[s] = weave.tile([P, S], F32, name="grad", tag="grad", bufs=4, align_bytes=64)
            for i, bank in enumerate(pair):
                for a in range(PASSES):
                    nc.tensor.matmul_mx(
                        out=bank[:],
                        lhsT=w[:, a, 2 * P * b : 2 * P * (b + 1)].bitcast(FP4X4),
                        lhsT_scale=ws[:, a, P * b : P * (b + 1)],
                        rhs=vwords[a][i].bitcast(FP8X4),
                        rhs_scale=vscale[a][:, BANK * i : BANK * (i + 1)],
                        start=(a == 0),
                        stop=(a == PASSES - 1),
                    )
                nc.scalar.activation(grads[s][:, BANK * i : BANK * (i + 1)], bank[:], IDENT, scale=-1.0)

        expand(0, banks[0:2])
        expand(1, banks[2:4])
        expand(2, banks[4:6])

        zt = [[kept(f"zt_{c}", [P, 4, BANK], BF16) for c in range(CHUNKS)]]
        ztw = [kept(f"ztw{c}", [P, 4, P, 2], BF16) for c in range(CHUNKS)]
        halves = [kept(f"halves{c}", [P, 2, BANK], F32) for c in range(CHUNKS)]
        turned = [kept(f"turned{c}", [P, 4, P], F32) for c in range(CHUNKS)]
        factor = {s: steps[:] for s in range(4)}

        def dealt(x, slot):
            return x.rearrange("(g t i) c -> t g i c", t=4, i=4)[slot]

        factors = reuse.tile([P, 4, S], F32, name="factors", align_bytes=64, offset=12288)

        def load_factor(s):
            factor[s] = factors[:, s - 4, :]
            for m in range(4):
                nc.sync.dma_start(factors[32 * m : 32 * (m + 1), s - 4, :], dealt(wgs, SLOT[s - 4]))

        zcodes = [[kept(f"zcodes{g}_{c}", [P, BANK], U32) for c in range(CHUNKS)] for g in range(PASSES)]
        zscale = [[kept(f"zscale{g}_{c}", [P, BANK], U8) for c in range(CHUNKS)] for g in range(PASSES)]
        dcodes = [kept(f"dcodes{g}", [P, N], U32) for g in range(PASSES)]
        dscale = [kept(f"dscale{g}", [P, N], U8) for g in range(PASSES)]
        result = [[kept(f"result{c}_{n}", [P, BANK], F32) for n in range(NT)] for c in range(CHUNKS)]
        olds = {}
        woven = {}

        def load_old(s):
            olds[s] = rows.tile([P, T2], F32, name="rowtile", tag="rows", align_bytes=64)
            nc.sync.dma_start(olds[s][:], old[P * s : P * (s + 1), :] if s < 4 else dealt(old[BANK:, :], SLOT[s - 4]))

        def quantise_dec(g):
            raw = rows.tile([P, 4, N], F32, name="rowtile", tag="rows", align_bytes=64)
            if g == 0:
                nc.sync.dma_start(raw[:], dec[:BANK, :].rearrange("(p j) n -> p j n", j=4))
            else:
                for slot in range(4):
                    nc.sync.dma_start(raw[:, slot, :], dealt(dec[BANK:, :], slot))
            grouped = weave.tile([P, 4 * N], BF16, name="woven", align_bytes=64)
            nc.scalar.copy(
                grouped[:].rearrange("p (c i j) -> p c j i", i=4, j=4),
                raw[:].rearrange("p j (c i) -> p c j i", i=4),
            )
            nc.vector.quantize_mx(out=dcodes[g][:].bitcast(FP8X4), scales=dscale[g][:], in_=grouped[:])

        def scatter(s):
            nc.vector.tensor_tensor(pages[s % 2][:].indirect(place[:]), grads[s][:], factor[s], MULT)

        def turn(source, c, first):
            for j in range(4):
                t0 = BANK * c + P * j
                nc.tensor.matmul(
                    banks[c][:, P * j : P * (j + 1)],
                    source[:, t0 : t0 + P],
                    ident[:],
                    start=(first and j == 0),
                    stop=(not first and j == 3),
                    is_transpose=True,
                )

        def round_rows(s, c):
            g, b = divmod(s, 4)
            nc.scalar.copy(
                zt[g][c][:].rearrange("t j (u b p e) -> t j b u p e", u=2, b=4, e=2)[:, :, b],
                banks[c][:].rearrange("t (j p u e) -> t j u p e", j=4, u=2, e=2),
            )

        def turn_back(g, c, half, bank):
            words = zt[g][c][:].bitcast(F32)
            for u in range(2):
                for jj in range(2):
                    o = 256 * u + P * jj
                    nc.tensor.transpose(bank[:, o : o + P], words[:, 2 * half + jj, P * u : P * (u + 1)], ident[:])

        def interleave(g, c, half, bank, on_vector):
            if half == 0:
                woven[g, c] = weave.tile([P, 4 * BANK], BF16, name="woven", align_bytes=64)
            dst = woven[g, c][:].bitcast(F32)[:, BANK * half : BANK * (half + 1)].rearrange("p (t u) -> p t u", u=2)
            src = bank[:].rearrange("p (u t) -> p t u", u=2)
            if on_vector:
                nc.vector.tensor_copy(dst, src)
            else:
                nc.scalar.copy(dst, src)

        def quantise(g, c):
            nc.vector.quantize_mx(out=zcodes[g][c][:].bitcast(FP8X4), scales=zscale[g][c][:], in_=woven[g, c][:])

        def decode(g, c, n, acc, start, stop, cols=slice(0, BANK)):
            nc.tensor.matmul_mx(
                out=acc,
                lhsT=dcodes[g][:, P * n : P * (n + 1)].bitcast(FP8X4),
                lhsT_scale=dscale[g][:, P * n : P * (n + 1)],
                rhs=zcodes[g][c][:, cols].bitcast(FP8X4),
                rhs_scale=zscale[g][c][:, cols],
                start=start,
                stop=stop,
            )

        def with_bias(c, n, bank):
            nc.scalar.activation(result[c][n][:], bank[:], IDENT, bias=bias[:, n : n + 1])

        def second_half(c):
            return halves[c][:, 1, :].bitcast(BF16).rearrange("p (t e) -> p t e", e=2)

        def back(source, c):
            for j in range(4):
                nc.tensor.transpose(banks[4 + c][:, P * j : P * (j + 1)], source[:, j, :], ident[:])

        units = [(0, 0, 256), (0, 256, 512), (1, 0, 512), (2, 0, 512), (3, 0, 256), (3, 256, 512)]

        def sums(unit):
            c, lo, hi = unit
            width = hi - lo
            share = BANK // width
            first = 4 * (c % 2) + 4 * lo // BANK
            return [banks[first + n // share][:, width * (n % share) : width * (n % share + 1)] for n in range(NT)]

        def multiply(g, unit):
            c, lo, hi = unit
            share = BANK // (hi - lo)
            for n, acc in enumerate(sums(unit)):
                decode(g, c, n, acc, g == 0 and n % share == 0, g == 1 and n % share == share - 1, slice(lo, hi))

        last = SLICES - 1
        load_old(0)
        for s in range(last):
            load_old(s + 1)
            for c in range(CHUNKS):
                turn(olds[s], c, True)
            scatter(s)
            if s < 4:
                load_factor(s + 4)
            for c in range(CHUNKS):
                turn(pages[s % 2], c, False)
                if s < 4:
                    round_rows(s, c)
                elif s == 6:
                    nc.scalar.copy(turned[c][:].rearrange("t j p -> t (j p)"), banks[c][:])
                else:
                    nc.scalar.copy(ztw[c][:, :, :, s - 4], banks[c][:].rearrange("t (j p) -> t j p", j=4))
            if s < 4:
                expand(s + 3, banks[2:4])
            if s == 5:
                expand(last, banks[2:4])
                for c in range(CHUNKS):
                    back(ztw[c][:].rearrange("t j p e -> t j (p e)").bitcast(F32), c)
                    nc.scalar.copy(halves[c][:, 0, :], banks[4 + c][:])
            if s == 6:
                for c in range(CHUNKS):
                    back(turned[c], c)
                    nc.scalar.copy(second_half(c), banks[4 + c][:].unsqueeze(2).to_broadcast([P, BANK, 2]))
            if s in (0, 1):
                quantise_dec(s)
            if s == 2:
                with nc.allow_non_contiguous_dma(reason="one bias value a partition"):
                    nc.sync.dma_start(bias[:], bd.rearrange("(n p) -> p n", p=P))
            if s == 3:
                for c in range(CHUNKS):
                    for half in range(2):
                        bank = banks[(4 + 2 * c + half) % 8]
                        turn_back(0, c, half, bank)
                        interleave(0, c, half, bank, False)
                    quantise(0, c)
        for unit in units[:3]:
            multiply(0, unit)
        scatter(last)

        ready = {}

        def subtract(unit):
            c, lo, hi = unit
            cols = slice(BANK * c + lo, BANK * c + hi)
            nc.vector.tensor_tensor(second_half(c)[:, lo:hi, 1], olds[last][:, cols], pages[last % 2][:, cols], ADD)

        def join(unit):
            c, lo, hi = unit
            ready[unit] = weave.tile([P, 4 * (hi - lo)], BF16, name="ready", tag="woven", align_bytes=64)
            nc.vector.tensor_copy(
                ready[unit][:].bitcast(F32).rearrange("p (t u) -> p t u", u=2),
                halves[c][:, :, lo:hi].rearrange("p u t -> p t u"),
            )

        def finish(unit):
            c, lo, hi = unit
            width = hi - lo
            share = BANK // width
            nc.vector.quantize_mx(
                out=zcodes[1][c][:, lo:hi].bitcast(FP8X4), scales=zscale[1][c][:, lo:hi], in_=ready[unit][:]
            )
            multiply(1, unit)
            for n, acc in enumerate(sums(unit)):
                staged = result[c][4 * lo // BANK + n // share]
                part = staged[:, width * (n % share) : width * (n % share + 1)]
                if c == CHUNKS - 1 and n >= 2:
                    nc.vector.tensor_scalar_add(part, acc, bias[:, n : n + 1])
                else:
                    nc.scalar.activation(part, acc, IDENT, bias=bias[:, n : n + 1])
                if n % share == share - 1:
                    nc.sync.dma_start(
                        out[P * (n + 1 - share) : P * (n + 1), BANK * c + lo : BANK * c + hi].rearrange(
                            "(k p) t -> p k t", p=P
                        ),
                        staged[:].rearrange("p (k t) -> p k t", k=share),
                    )
            if hi == BANK:
                for later in units:
                    if later[0] == c + 2:
                        multiply(0, later)

        subtract(units[0])
        subtract(units[1])
        join(units[0])
        join(units[1])
        finish(units[0])
        for i in range(1, len(units)):
            if i + 1 < len(units):
                subtract(units[i + 1])
            finish(units[i])
            if i + 1 < len(units):
                join(units[i + 1])
